import numpy as np
import ml_dtypes


def mxq(x, axis, fmt="e4m3"):
    dtype, down = {"e4m3": (ml_dtypes.float8_e4m3fn, 7), "e5m2": (ml_dtypes.float8_e5m2, 14)}[fmt]
    v = np.moveaxis(np.asarray(x, np.float32).astype(ml_dtypes.bfloat16).astype(np.float64), axis, -1)
    blocks = v.reshape(v.shape[:-1] + (-1, 32))
    amax = np.abs(blocks).max(-1, keepdims=True)
    byte = np.maximum(np.where(amax > 0, np.frexp(amax)[1] - 1 + 127, 0) - down, 1)
    scale = np.exp2(byte - 127.0)
    codes = (blocks / scale).astype(np.float32).astype(dtype).astype(np.float64)
    return np.moveaxis((codes * scale).reshape(v.shape), -1, axis)


WIDE = False


def mx_kscale(k):
    if not WIDE:
        return np.ones(k)
    levels = np.array([10, -10, 5, -5, 0])
    if k % 512:
        return np.exp2(np.random.permutation(np.resize(levels, k // 32))).repeat(32)
    a = np.empty((k // 512, 16))
    for p in range(k // 512):
        a[p, :8] = np.random.permutation(np.resize(levels, 8))
        for g in range(8):
            far = levels[np.abs(levels - a[p, g]) >= 10]
            a[p, g + 8] = far[np.random.randint(len(far))]
    return np.exp2(a.ravel()).repeat(32)


def f64(x):
    return np.asarray(x).astype(np.float64)


def striped(idx):
    return np.tile(idx.reshape(-1, 16).T, (8, 1)).astype(np.uint16)


def unstriped(offs):
    return offs[:16].T.reshape(-1).astype(np.int64)


def pack_weight(w):
    k, n = w.shape
    w = f64(np.asarray(w, np.float32).astype(ml_dtypes.bfloat16)).reshape(k // 32, 32, n)
    amax = np.abs(w).max(1)
    byte = np.clip(np.where(amax > 0, np.frexp(amax)[1] - 1 + 127 - 7, 1), 1, 254)
    scaled = (w * np.exp2(127.0 - byte)[:, None, :]).reshape(k, n).astype(np.float32)
    words = np.ascontiguousarray(scaled.reshape(k // 512, 128, 4, n).transpose(0, 1, 3, 2)).astype(ml_dtypes.float8_e4m3fn).view(np.uint8)
    return words, np.ascontiguousarray(byte.astype(np.uint8).reshape(k // 512, 16, n))


def unpack_weight(words, scales):
    g, p, n, _ = words.shape
    vals = np.ascontiguousarray(words).view(ml_dtypes.float8_e4m3fn).astype(np.float64) * np.repeat(np.exp2(scales.astype(np.float64) - 127.0), 8, axis=1)[..., None]
    return vals.transpose(0, 1, 3, 2).reshape(g * 512, n)


def sigmoid(v):
    return 1.0 / (1.0 + np.exp(-np.maximum(v, -700.0)))


K, T, S, N, H = 1024, 2048, 512, 128, 512


def setup_inputs():
    n = np.random.standard_normal
    s = mx_kscale(K)[:, None]
    u = mx_kscale(H)
    packed_xT = pack_weight(n((K, T)) * s)
    return {
        "x_words": packed_xT[0],
        "x_scales": packed_xT[1],
        "w1": (n((K, H)) / np.sqrt(K) / s).astype(np.float32),
        "w2": (n((K, H)) / np.sqrt(K) / s).astype(np.float32),
        "unit": (np.random.uniform(0.6, 1.4, (H, 1)) * u[:, None]).astype(np.float32),
        "w3": (n((H, N)) / np.sqrt(H) / u[:, None]).astype(np.float32),
        "offs": striped(np.random.permutation(T)[:S]),
        "wrp": striped(np.random.permutation(S)),
        "wr2": striped(np.random.permutation(S)),
    }


def reference(x_words, x_scales, w1, w2, unit, w3, offs, wrp, wr2):
    xq = unpack_weight(x_words, x_scales)[:, unstriped(offs)]
    fu = mxq(f64(w1), 0, "e4m3").T @ xq
    fw = np.tanh(fu)
    bu = mxq(f64(w2), 0, "e4m3").T @ xq
    bv = np.tanh(bu)
    bw = bv[:, unstriped(wrp)]
    inc = fw + bw
    occ = sigmoid(4.0 * ((inc) ** 2 - (0.3 * ((fw) ** 2 + (bw) ** 2)) - 0.2))
    f2 = fw[:, unstriped(wr2)]
    comp = f2 - fw
    fix = (-1.0 * occ + 1.0) * fw + occ * comp
    hid = f64(unit) * fix
    return mxq(f64(w3), 0, "e4m3").T @ mxq(hid, 0, "e4m3")

@@ -1,0 +1,226 @@
+import math
+from contextlib import ExitStack
+
+import concourse.mybir as mybir
+
+K, T, S, N, H = 1024, 2048, 512, 128, 512
+FLOPS = 2 * (2 * K * H * S + H * N * S)
+
+F32 = mybir.dt.float32
+BF16 = mybir.dt.bfloat16
+I32 = mybir.dt.int32
+U32 = mybir.dt.uint32
+U16 = mybir.dt.uint16
+U8 = mybir.dt.uint8
+FP8X4 = mybir.dt.float8_e4m3fn_x4
+ALU = mybir.AluOpType
+ACT = mybir.ActivationFunctionType
+
+P = 128
+PACK = 4
+PASSES = K // (P * PACK)
+HALF = S // 2
+LIST_HALF = HALF // 16
+
+ROOT = (1.0 + math.sqrt(1.0 - 0.7 * 0.7)) / 0.7
+
+
+def tile_picked_yfbflo_fix_p_kernel(tc, x_words, x_scales, w1, w2, unit, w3, offs, wrp, wr2, out):
+    nc = tc.nc
+    with ExitStack() as ctx:
+        keep = ctx.enter_context(tc.tile_pool(name="keep", bufs=1))
+        psum = ctx.enter_context(tc.psum_pool(name="psum", bufs=1))
+
+        offs_sb = keep.tile([P, S // 16], U16, name="offs_sb")
+        wrp_sb = keep.tile([P, S // 16], U16, name="wrp_sb")
+        wr2_sb = keep.tile([P, S // 16], U16, name="wr2_sb")
+        table_words = [keep.tile([P, T], I32, name="table_words%d" % g) for g in range(PASSES)]
+        table_scales = keep.tile([P, T], U8, name="table_scales")
+        x_codes = [keep.tile([P, S], U32, name="x_codes%d" % g, align_bytes=64) for g in range(PASSES)]
+        x_planes = keep.tile([P, S], U8, name="x_planes", align_bytes=64)
+
+        def load_words(g):
+            nc.sync.dma_start(table_words[g][:], x_words[g].rearrange("p c r -> p (c r)").bitcast(I32))
+
+        def load_weight(w, name, g, c0, c1):
+            raw = keep.tile([P, PACK, c1 - c0], F32, name="raw_%s_%d_%d" % (name, g, c0), align_bytes=64)
+            rows = w[g * P * PACK : (g + 1) * P * PACK, :].rearrange("(p j) c -> p j c", j=PACK)
+            nc.sync.dma_start(raw[:], rows[:, :, c0:c1])
+            return raw
+
+        nc.vector.memset(table_scales[:].bitcast(I32), 0)
+        load_words(0)
+        nc.sync.dma_start(offs_sb[:], offs)
+        for q in range(4):
+            nc.sync.dma_start(
+                table_scales[32 * q : 32 * q + 4 * PASSES, :].bitcast(I32),
+                x_scales[:, 4 * q : 4 * q + 4, :].bitcast(I32),
+            )
+        w1_first = [load_weight(w1, "w1", 0, 0, H)]
+        load_words(1)
+        w1_last = [load_weight(w1, "w1", 1, c0, c0 + H // 2) for c0 in (0, H // 2)]
+        nc.sync.dma_start(wr2_sb[:], wr2)
+        w2_first = [load_weight(w2, "w2", 0, c0, c0 + H // 2) for c0 in (0, H // 2)]
+        nc.sync.dma_start(wrp_sb[:], wrp)
+        w2_last = [load_weight(w2, "w2", 1, c0, c0 + H // 2) for c0 in (0, H // 2)]
+        unit_sb = keep.tile([P, PACK], F32, name="unit_sb")
+        nc.sync.dma_start(unit_sb[:], unit.rearrange("(p t) o -> p (t o)", t=PACK))
+        w3_raw = load_weight(w3, "w3", 0, 0, N)
+
+        def deal(copy, dealt, raw, c0, m0, m1):
+            src = raw[:, :, PACK * m0 - c0 : PACK * m1 - c0].rearrange("p j (m t) -> p m j t", t=PACK)
+            copy(dealt[:, :, m0:m1, :].rearrange("p t m j -> p m j t"), src)
+
+        def mx_tiles(name, width):
+            codes = keep.tile([P, width], U32, name=name + "_codes", align_bytes=64)
+            plane = keep.tile([P, width], U8, name=name + "_plane", align_bytes=64)
+            return codes, plane
+
+        def quantise(mx, c0, c1, values):
+            nc.vector.quantize_mx(out=mx[0][:, c0:c1].bitcast(FP8X4), scales=mx[1][:, c0:c1], in_=values)
+
+        def product_pass(bank, w_mx, t, g):
+            cols = slice(t * P, (t + 1) * P)
+            nc.tensor.matmul_mx(
+                out=bank[:],
+                lhsT=w_mx[0][:, cols].bitcast(FP8X4),
+                lhsT_scale=w_mx[1][:, cols],
+                rhs=x_codes[g][:].bitcast(FP8X4),
+                rhs_scale=x_planes[4 * g :, :],
+                start=(g == 0),
+                stop=(g == PASSES - 1),
+            )
+
+        def gather_words(g):
+            nc.vector.tensor_copy(x_codes[g][:], table_words[g][:].bitcast(U32).indirect(offs_sb[:]))
+
+        def dealt_tile(name):
+            return keep.tile([P, PACK, P, PACK], BF16, name=name, align_bytes=64)
+
+        def first_pass(raws, name, banks):
+            dealt = dealt_tile(name + "_dealt0")
+            share = P // len(raws)
+            for a, raw in enumerate(raws):
+                deal(nc.vector.tensor_copy, dealt, raw, PACK * a * share, a * share, (a + 1) * share)
+            mx = mx_tiles(name + "_0", H)
+            quantise(mx, 0, H, dealt[:].rearrange("p t m j -> p (t m j)"))
+            for t in range(PACK):
+                product_pass(banks[t], mx, t, 0)
+
+        def last_pass(raws, name, banks):
+            dealt = dealt_tile(name + "_dealt1")
+            deal(nc.vector.tensor_copy, dealt, raws[0], 0, 0, P // 2)
+            deal(nc.vector.tensor_copy, dealt, raws[1], H // 2, P // 2, P)
+            mx = mx_tiles(name + "_1", H)
+            for t in range(PACK):
+                quantise(mx, t * P, (t + 1) * P, dealt[:, t].rearrange("p m j -> p (m j)"))
+                product_pass(banks[t], mx, t, 1)
+
+        fu = [psum.tile([P, S], F32, name="fu%d" % t, tag="bank%d" % t) for t in range(PACK)]
+        bu = [psum.tile([P, S], F32, name="bu%d" % t, tag="bank%d" % (PACK + t)) for t in range(PACK)]
+
+        nc.vector.tensor_copy(x_planes[:], table_scales[:].indirect(offs_sb[:]))
+        gather_words(0)
+        first_pass(w1_first, "w1", fu)
+        gather_words(1)
+        last_pass(w1_last, "w1", fu)
+
+        def row_tile(name, t, tag=None):
+            name = "%s%d" % (name, t)
+            return keep.tile([P, S], F32, name=name, tag=tag or name, align_bytes=64)
+
+        def fetch(dst, window, places):
+            for a in range(2):
+                nc.scalar.activation(
+                    dst[:, a * HALF : (a + 1) * HALF],
+                    window[:].indirect(places[:, a * LIST_HALF : (a + 1) * LIST_HALF]),
+                    ACT.Copy,
+                )
+
+        fw = [row_tile("fw", t) for t in range(PACK)]
+        for t in range(PACK):
+            nc.scalar.activation(fw[t][:], fu[t][:], ACT.Tanh)
+
+        first_pass(w2_first, "w2", bu)
+        last_pass(w2_last, "w2", bu)
+
+        half_unit = keep.tile([P, PACK], F32, name="half_unit")
+        nc.vector.tensor_scalar(half_unit[:], unit_sb[:], 0.5, None, ALU.mult)
+
+        bv = {}
+        bv_tag = ["bv0", "bv1", "form0", "form1"]
+        bw = [row_tile("bw", t) for t in range(PACK)]
+        f2 = {}
+        gap = [row_tile("gap", t, {0: "w2_dealt1", 1: "raw_w2_1_256"}.get(t)) for t in range(PACK)]
+        lead = [row_tile("lead", t) for t in range(PACK)]
+        trail = [row_tile("trail", t) for t in range(PACK)]
+        form = [row_tile("form", t) for t in range(PACK)]
+        tau = [row_tile("tau", t) for t in range(PACK)]
+        swing = [row_tile("swing", t) for t in range(PACK)]
+        hid = [keep.tile([P, PACK, HALF], BF16, name="hid%d" % a) for a in range(2)]
+
+        def forward_fetch(t):
+            f2[t] = row_tile("f2", t, bv_tag[t - 1] if t >= 2 else None)
+            fetch(f2[t], fw[t], wr2_sb)
+            nc.vector.scalar_tensor_tensor(gap[t][:], fw[t][:], -2.0, f2[t][:], ALU.mult, ALU.add)
+
+        def occlusion(t, cols):
+            nc.vector.scalar_tensor_tensor(lead[t][:, cols], bw[t][:, cols], ROOT, fw[t][:, cols], ALU.mult, ALU.add)
+            nc.vector.scalar_tensor_tensor(trail[t][:, cols], bw[t][:, cols], 1.0 / ROOT, fw[t][:, cols], ALU.mult, ALU.add)
+            nc.vector.tensor_tensor(form[t][:, cols], lead[t][:, cols], trail[t][:, cols], ALU.mult)
+            nc.scalar.activation(tau[t][:, cols], form[t][:, cols], ACT.Tanh, scale=1.4, bias=-0.4)
+
+        def repair(t, halves):
+            cols = slice(halves[0] * HALF, (halves[-1] + 1) * HALF)
+            u = half_unit[:, t : t + 1]
+            nc.vector.scalar_tensor_tensor(swing[t][:, cols], gap[t][:, cols], u, tau[t][:, cols], ALU.mult, ALU.mult)
+            for a in halves:
+                part = slice(a * HALF, (a + 1) * HALF)
+                nc.vector.scalar_tensor_tensor(hid[a][:, t, :], f2[t][:, part], u, swing[t][:, part], ALU.mult, ALU.add)
+
+        forward_fetch(0)
+        forward_fetch(1)
+        for t in range(PACK):
+            bv[t] = row_tile("bv", t, bv_tag[t])
+            nc.scalar.activation(bv[t][:], bu[t][:], ACT.Tanh)
+            fetch(bw[t], bv[t], wrp_sb)
+            if t < PACK - 1:
+                occlusion(t, slice(0, S))
+            else:
+                occlusion(t, slice(0, HALF))
+                occlusion(t, slice(HALF, S))
+            if t >= 2:
+                forward_fetch(t)
+            if t >= 1:
+                repair(t - 1, (0, 1))
+
+        w3_dealt = keep.tile([P, N, PACK], BF16, name="w3_dealt", tag="bv0", align_bytes=64)
+        nc.scalar.copy(
+            w3_dealt[:].rearrange("p (c i) j -> p c j i", i=4),
+            w3_raw[:].rearrange("p j (c i) -> p c j i", i=4),
+        )
+        w3_mx = mx_tiles("w3", N)
+        quantise(w3_mx, 0, N, w3_dealt[:].rearrange("p n j -> p (n j)"))
+
+        for a, copy in ((0, nc.scalar.copy), (1, nc.vector.tensor_copy)):
+            repair(PACK - 1, (a,))
+            woven = keep.tile([P, HALF, PACK], BF16, name="woven%d" % a, align_bytes=64)
+            copy(
+                woven[:].rearrange("p (c i) t -> p c t i", i=4),
+                hid[a][:].rearrange("p t (c i) -> p c t i", i=4),
+            )
+            hid_mx = mx_tiles("hid%d" % a, HALF)
+            quantise(hid_mx, 0, HALF, woven[:].rearrange("p c t -> p (c t)"))
+            motion = psum.tile([P, HALF], F32, name="motion%d" % a, tag="bank%d" % a)
+            nc.tensor.matmul_mx(
+                out=motion[:],
+                lhsT=w3_mx[0][:].bitcast(FP8X4),
+                lhsT_scale=w3_mx[1][:],
+                rhs=hid_mx[0][:].bitcast(FP8X4),
+                rhs_scale=hid_mx[1][:],
+                start=True,
+                stop=True,
+            )
+            result = keep.tile([P, HALF], F32, name="result%d" % a)
+            nc.scalar.copy(result[:], motion[:])
+            nc.sync.dma_start(out[:, a * HALF : (a + 1) * HALF], result[:])

@@ -19,25 +19,29 @@ ACT = mybir.ActivationFunctionType
 P = 128
 PACK = 4
 PASSES = K // (P * PACK)
+TILES = H // P
+QUADRANT = 32
+PLANE_ROWS = 4
+LIST_ROWS = 16
 HALF = S // 2
-LIST_HALF = HALF // 16
-
+RUN = 4
+EARLY = 2
 ROOT = (1.0 + math.sqrt(1.0 - 0.7 * 0.7)) / 0.7
 
 
-def tile_picked_yfbflo_fix_p_kernel(tc, x_words, x_scales, w1, w2, unit, w3, offs, wrp, wr2, out):
+def tile_picked_yfbflo_fix_p_kernel(
+    tc, x_words, x_scales, w1, w2, unit, w3, offs, wrp, wr2, out
+):
     nc = tc.nc
     with ExitStack() as ctx:
         keep = ctx.enter_context(tc.tile_pool(name="keep", bufs=1))
         psum = ctx.enter_context(tc.psum_pool(name="psum", bufs=1))
 
-        offs_sb = keep.tile([P, S // 16], U16, name="offs_sb")
-        wrp_sb = keep.tile([P, S // 16], U16, name="wrp_sb")
-        wr2_sb = keep.tile([P, S // 16], U16, name="wr2_sb")
+        offs_sb = keep.tile([P, S // LIST_ROWS], U16, name="offs_sb")
+        wrp_sb = keep.tile([P, S // LIST_ROWS], U16, name="wrp_sb")
+        wr2_sb = keep.tile([P, S // LIST_ROWS], U16, name="wr2_sb")
         table_words = [keep.tile([P, T], I32, name="table_words%d" % g) for g in range(PASSES)]
         table_scales = keep.tile([P, T], U8, name="table_scales")
-        x_codes = [keep.tile([P, S], U32, name="x_codes%d" % g, align_bytes=64) for g in range(PASSES)]
-        x_planes = keep.tile([P, S], U8, name="x_planes", align_bytes=64)
 
         def load_words(g):
             nc.sync.dma_start(table_words[g][:], x_words[g].rearrange("p c r -> p (c r)").bitcast(I32))
@@ -48,28 +52,30 @@ def tile_picked_yfbflo_fix_p_kernel(tc, x_words, x_scales, w1, w2, unit, w3, off
             nc.sync.dma_start(raw[:], rows[:, :, c0:c1])
             return raw
 
+        def load_halves(w, name, g):
+            return [load_weight(w, name, g, c0, c0 + H // 2) for c0 in (0, H // 2)]
+
         nc.vector.memset(table_scales[:].bitcast(I32), 0)
         load_words(0)
         nc.sync.dma_start(offs_sb[:], offs)
-        for q in range(4):
+        for q in range(P // QUADRANT):
             nc.sync.dma_start(
-                table_scales[32 * q : 32 * q + 4 * PASSES, :].bitcast(I32),
-                x_scales[:, 4 * q : 4 * q + 4, :].bitcast(I32),
+                table_scales[QUADRANT * q : QUADRANT * q + PLANE_ROWS * PASSES, :].bitcast(I32),
+                x_scales[:, PLANE_ROWS * q : PLANE_ROWS * (q + 1), :].bitcast(I32),
             )
         w1_first = [load_weight(w1, "w1", 0, 0, H)]
         load_words(1)
-        w1_last = [load_weight(w1, "w1", 1, c0, c0 + H // 2) for c0 in (0, H // 2)]
+        w1_last = load_halves(w1, "w1", 1)
         nc.sync.dma_start(wr2_sb[:], wr2)
-        w2_first = [load_weight(w2, "w2", 0, c0, c0 + H // 2) for c0 in (0, H // 2)]
+        w2_first = load_halves(w2, "w2", 0)
         nc.sync.dma_start(wrp_sb[:], wrp)
-        w2_last = [load_weight(w2, "w2", 1, c0, c0 + H // 2) for c0 in (0, H // 2)]
-        unit_sb = keep.tile([P, PACK], F32, name="unit_sb")
-        nc.sync.dma_start(unit_sb[:], unit.rearrange("(p t) o -> p (t o)", t=PACK))
+        w2_last = load_halves(w2, "w2", 1)
+        unit_sb = keep.tile([P, TILES], F32, name="unit_sb")
+        nc.sync.dma_start(unit_sb[:], unit.rearrange("(p t) o -> p (t o)", t=TILES))
         w3_raw = load_weight(w3, "w3", 0, 0, N)
 
-        def deal(copy, dealt, raw, c0, m0, m1):
-            src = raw[:, :, PACK * m0 - c0 : PACK * m1 - c0].rearrange("p j (m t) -> p m j t", t=PACK)
-            copy(dealt[:, :, m0:m1, :].rearrange("p t m j -> p m j t"), src)
+        x_codes = [keep.tile([P, S], U32, name="x_codes%d" % g, align_bytes=64) for g in range(PASSES)]
+        x_planes = keep.tile([P, S], U8, name="x_planes", align_bytes=64)
 
         def mx_tiles(name, width):
             codes = keep.tile([P, width], U32, name=name + "_codes", align_bytes=64)
@@ -77,47 +83,55 @@ def tile_picked_yfbflo_fix_p_kernel(tc, x_words, x_scales, w1, w2, unit, w3, off
             return codes, plane
 
         def quantise(mx, c0, c1, values):
-            nc.vector.quantize_mx(out=mx[0][:, c0:c1].bitcast(FP8X4), scales=mx[1][:, c0:c1], in_=values)
-
-        def product_pass(bank, w_mx, t, g):
-            cols = slice(t * P, (t + 1) * P)
-            nc.tensor.matmul_mx(
-                out=bank[:],
-                lhsT=w_mx[0][:, cols].bitcast(FP8X4),
-                lhsT_scale=w_mx[1][:, cols],
-                rhs=x_codes[g][:].bitcast(FP8X4),
-                rhs_scale=x_planes[4 * g :, :],
-                start=(g == 0),
-                stop=(g == PASSES - 1),
-            )
+            codes, plane = mx
+            nc.vector.quantize_mx(out=codes[:, c0:c1].bitcast(FP8X4), scales=plane[:, c0:c1], in_=values)
 
         def gather_words(g):
             nc.vector.tensor_copy(x_codes[g][:], table_words[g][:].bitcast(U32).indirect(offs_sb[:]))
 
-        def dealt_tile(name):
-            return keep.tile([P, PACK, P, PACK], BF16, name=name, align_bytes=64)
-
-        def first_pass(raws, name, banks):
-            dealt = dealt_tile(name + "_dealt0")
+        def deal(raws, name):
+            dealt = keep.tile([P, TILES, P, PACK], BF16, name=name, align_bytes=64)
             share = P // len(raws)
             for a, raw in enumerate(raws):
-                deal(nc.vector.tensor_copy, dealt, raw, PACK * a * share, a * share, (a + 1) * share)
+                nc.vector.tensor_copy(
+                    dealt[:, :, a * share : (a + 1) * share, :].rearrange("p t m j -> p m j t"),
+                    raw[:].rearrange("p j (m t) -> p m j t", t=TILES),
+                )
+            return dealt
+
+        def product_pass(bank, w_mx, t, g):
+            codes, plane = w_mx
+            cols = slice(t * P, (t + 1) * P)
+            nc.tensor.matmul_mx(
+                out=bank[:],
+                lhsT=codes[:, cols].bitcast(FP8X4),
+                lhsT_scale=plane[:, cols],
+                rhs=x_codes[g][:].bitcast(FP8X4),
+                rhs_scale=x_planes[PLANE_ROWS * g :, :],
+                start=(g == 0),
+                stop=(g == PASSES - 1),
+            )
+
+        def first_pass(raws, name, banks):
+            dealt = deal(raws, name + "_dealt0")
             mx = mx_tiles(name + "_0", H)
             quantise(mx, 0, H, dealt[:].rearrange("p t m j -> p (t m j)"))
-            for t in range(PACK):
+            for t in range(TILES):
                 product_pass(banks[t], mx, t, 0)
 
         def last_pass(raws, name, banks):
-            dealt = dealt_tile(name + "_dealt1")
-            deal(nc.vector.tensor_copy, dealt, raws[0], 0, 0, P // 2)
-            deal(nc.vector.tensor_copy, dealt, raws[1], H // 2, P // 2, P)
+            dealt = deal(raws, name + "_dealt1")
             mx = mx_tiles(name + "_1", H)
-            for t in range(PACK):
+            for t in range(TILES):
                 quantise(mx, t * P, (t + 1) * P, dealt[:, t].rearrange("p m j -> p (m j)"))
                 product_pass(banks[t], mx, t, 1)
 
-        fu = [psum.tile([P, S], F32, name="fu%d" % t, tag="bank%d" % t) for t in range(PACK)]
-        bu = [psum.tile([P, S], F32, name="bu%d" % t, tag="bank%d" % (PACK + t)) for t in range(PACK)]
+        def row_tile(name, t, tag=None):
+            name = "%s%d" % (name, t)
+            return keep.tile([P, S], F32, name=name, tag=tag or name, align_bytes=64)
+
+        fu = [psum.tile([P, S], F32, name="fu%d" % t, tag="bank%d" % t) for t in range(TILES)]
+        bu = [psum.tile([P, S], F32, name="bu%d" % t, tag="bank%d" % (TILES + t)) for t in range(TILES)]
 
         nc.vector.tensor_copy(x_planes[:], table_scales[:].indirect(offs_sb[:]))
         gather_words(0)
@@ -125,92 +139,93 @@ def tile_picked_yfbflo_fix_p_kernel(tc, x_words, x_scales, w1, w2, unit, w3, off
         gather_words(1)
         last_pass(w1_last, "w1", fu)
 
-        def row_tile(name, t, tag=None):
-            name = "%s%d" % (name, t)
-            return keep.tile([P, S], F32, name=name, tag=tag or name, align_bytes=64)
-
-        def fetch(dst, window, places):
-            for a in range(2):
-                nc.scalar.activation(
-                    dst[:, a * HALF : (a + 1) * HALF],
-                    window[:].indirect(places[:, a * LIST_HALF : (a + 1) * LIST_HALF]),
-                    ACT.Copy,
-                )
-
-        fw = [row_tile("fw", t) for t in range(PACK)]
-        for t in range(PACK):
+        fw = [row_tile("fw", t) for t in range(TILES)]
+        for t in range(TILES):
             nc.scalar.activation(fw[t][:], fu[t][:], ACT.Tanh)
 
         first_pass(w2_first, "w2", bu)
         last_pass(w2_last, "w2", bu)
 
-        half_unit = keep.tile([P, PACK], F32, name="half_unit")
+        half_unit = keep.tile([P, TILES], F32, name="half_unit")
         nc.vector.tensor_scalar(half_unit[:], unit_sb[:], 0.5, None, ALU.mult)
 
-        bv = {}
-        bv_tag = ["bv0", "bv1", "form0", "form1"]
-        bw = [row_tile("bw", t) for t in range(PACK)]
-        f2 = {}
-        gap = [row_tile("gap", t, {0: "w2_dealt1", 1: "raw_w2_1_256"}.get(t)) for t in range(PACK)]
-        lead = [row_tile("lead", t) for t in range(PACK)]
-        trail = [row_tile("trail", t) for t in range(PACK)]
-        form = [row_tile("form", t) for t in range(PACK)]
-        tau = [row_tile("tau", t) for t in range(PACK)]
-        swing = [row_tile("swing", t) for t in range(PACK)]
-        hid = [keep.tile([P, PACK, HALF], BF16, name="hid%d" % a) for a in range(2)]
+        whole = slice(0, S)
+        halves = (slice(0, HALF), slice(HALF, S))
+        last = TILES - 1
+        f2, gap, tau, swing = {}, {}, {}, {}
+        hid = [keep.tile([P, TILES, HALF], BF16, name="hid%d" % a) for a in range(2)]
 
-        def forward_fetch(t):
-            f2[t] = row_tile("f2", t, bv_tag[t - 1] if t >= 2 else None)
-            fetch(f2[t], fw[t], wr2_sb)
-            nc.vector.scalar_tensor_tensor(gap[t][:], fw[t][:], -2.0, f2[t][:], ALU.mult, ALU.add)
+        def scalar_fetch(dst, picked):
+            nc.scalar.activation(dst, picked, ACT.Copy)
 
-        def occlusion(t, cols):
-            nc.vector.scalar_tensor_tensor(lead[t][:, cols], bw[t][:, cols], ROOT, fw[t][:, cols], ALU.mult, ALU.add)
-            nc.vector.scalar_tensor_tensor(trail[t][:, cols], bw[t][:, cols], 1.0 / ROOT, fw[t][:, cols], ALU.mult, ALU.add)
-            nc.vector.tensor_tensor(form[t][:, cols], lead[t][:, cols], trail[t][:, cols], ALU.mult)
-            nc.scalar.activation(tau[t][:, cols], form[t][:, cols], ACT.Tanh, scale=1.4, bias=-0.4)
+        def fetch(dst, window, places, copies):
+            width = HALF // LIST_ROWS
+            for a, copy in enumerate(copies):
+                copy(dst[:, halves[a]], window[:].indirect(places[:, a * width : (a + 1) * width]))
 
-        def repair(t, halves):
-            cols = slice(halves[0] * HALF, (halves[-1] + 1) * HALF)
-            u = half_unit[:, t : t + 1]
-            nc.vector.scalar_tensor_tensor(swing[t][:, cols], gap[t][:, cols], u, tau[t][:, cols], ALU.mult, ALU.mult)
-            for a in halves:
-                part = slice(a * HALF, (a + 1) * HALF)
-                nc.vector.scalar_tensor_tensor(hid[a][:, t, :], f2[t][:, part], u, swing[t][:, part], ALU.mult, ALU.add)
+        def stand_in(t, tag, difference):
+            f2[t] = row_tile("f2", t, tag)
+            fetch(f2[t], fw[t], wr2_sb, (scalar_fetch, scalar_fetch))
+            gap[t] = difference
+            nc.vector.scalar_tensor_tensor(gap[t][:, whole], fw[t][:], -2.0, f2[t][:], ALU.mult, ALU.add)
 
-        forward_fetch(0)
-        forward_fetch(1)
-        for t in range(PACK):
-            bv[t] = row_tile("bv", t, bv_tag[t])
-            nc.scalar.activation(bv[t][:], bu[t][:], ACT.Tanh)
-            fetch(bw[t], bv[t], wrp_sb)
-            if t < PACK - 1:
-                occlusion(t, slice(0, S))
-            else:
-                occlusion(t, slice(0, HALF))
-                occlusion(t, slice(HALF, S))
-            if t >= 2:
-                forward_fetch(t)
-            if t >= 1:
-                repair(t - 1, (0, 1))
+        def occlusion(t, bw, parts):
+            lead, trail, form = row_tile("lead", t), row_tile("trail", t), row_tile("form", t)
+            tau[t] = row_tile("tau", t)
+            for cols in parts:
+                nc.vector.scalar_tensor_tensor(lead[:, cols], bw[:, cols], ROOT, fw[t][:, cols], ALU.mult, ALU.add)
+                nc.vector.scalar_tensor_tensor(trail[:, cols], bw[:, cols], 1.0 / ROOT, fw[t][:, cols], ALU.mult, ALU.add)
+                nc.vector.tensor_tensor(form[:, cols], lead[:, cols], trail[:, cols], ALU.mult)
+                nc.scalar.activation(tau[t][:, cols], form[:, cols], ACT.Tanh, scale=1.4, bias=-0.4)
 
-        w3_dealt = keep.tile([P, N, PACK], BF16, name="w3_dealt", tag="bv0", align_bytes=64)
-        nc.scalar.copy(
-            w3_dealt[:].rearrange("p (c i) j -> p c j i", i=4),
-            w3_raw[:].rearrange("p j (c i) -> p c j i", i=4),
-        )
-        w3_mx = mx_tiles("w3", N)
-        quantise(w3_mx, 0, N, w3_dealt[:].rearrange("p n j -> p (n j)"))
-
-        for a, copy in ((0, nc.scalar.copy), (1, nc.vector.tensor_copy)):
-            repair(PACK - 1, (a,))
-            woven = keep.tile([P, HALF, PACK], BF16, name="woven%d" % a, align_bytes=64)
-            copy(
-                woven[:].rearrange("p (c i) t -> p c t i", i=4),
-                hid[a][:].rearrange("p t (c i) -> p c t i", i=4),
+        def gate(t, cols):
+            nc.vector.scalar_tensor_tensor(
+                swing[t][:, cols], gap[t][:, cols], half_unit[:, t : t + 1], tau[t][:, cols], ALU.mult, ALU.mult
             )
+
+        def repair(t, a):
+            nc.vector.scalar_tensor_tensor(
+                hid[a][:, t, :], f2[t][:, halves[a]], half_unit[:, t : t + 1], swing[t][:, halves[a]], ALU.mult, ALU.add
+            )
+
+        early_gaps = keep.tile([P, EARLY, S], F32, name="early_gaps", tag="w2_dealt1", align_bytes=64)
+        for t in range(EARLY):
+            stand_in(t, None, early_gaps[:, t, :])
+
+        bv_tags = ["bv%d" % t if t < EARLY else "form%d" % (t - EARLY) for t in range(TILES)]
+        for t in range(TILES):
+            bv = row_tile("bv", t, bv_tags[t])
+            nc.scalar.activation(bv[:], bu[t][:], ACT.Tanh)
+            bw = row_tile("bw", t)
+            fetch(bw, bv, wrp_sb, (scalar_fetch, nc.vector.tensor_copy if t == 0 else scalar_fetch))
+            occlusion(t, bw, halves if t == last else (whole,))
+            if t >= EARLY:
+                stand_in(t, bv_tags[t - 1], row_tile("gap", t))
+            swing[t] = row_tile("swing", t)
+            if 0 < t < last:
+                gate(t - 1, whole)
+                repair(t - 1, 0)
+                repair(t - 1, 1)
+
+        def interleave(copy, dst, src):
+            copy(dst.rearrange("p (c i) j -> p c j i", i=RUN), src.rearrange("p j (c i) -> p c j i", i=RUN))
+
+        w3_grouped = keep.tile([P, N, PACK], BF16, name="w3_grouped", tag="bw1", align_bytes=64)
+        interleave(nc.scalar.copy, w3_grouped[:], w3_raw[:])
+        w3_mx = mx_tiles("w3", N)
+        quantise(w3_mx, 0, N, w3_grouped[:].rearrange("p n j -> p (n j)"))
+
+        woven = [keep.tile([P, HALF, TILES], BF16, name="woven%d" % a, align_bytes=64) for a in range(2)]
+        gate(last - 1, whole)
+        for a, copy in enumerate((nc.scalar.copy, nc.vector.tensor_copy)):
+            gate(last, halves[a])
+            repair(last - 1, a)
+            repair(last, a)
+            interleave(copy, woven[a][:], hid[a][:])
+
+        for a in range(2):
             hid_mx = mx_tiles("hid%d" % a, HALF)
-            quantise(hid_mx, 0, HALF, woven[:].rearrange("p c t -> p (c t)"))
+            quantise(hid_mx, 0, HALF, woven[a][:].rearrange("p c t -> p (c t)"))
             motion = psum.tile([P, HALF], F32, name="motion%d" % a, tag="bank%d" % a)
             nc.tensor.matmul_mx(
                 out=motion[:],
@@ -223,4 +238,4 @@ def tile_picked_yfbflo_fix_p_kernel(tc, x_words, x_scales, w1, w2, unit, w3, off
             )
             result = keep.tile([P, HALF], F32, name="result%d" % a)
             nc.scalar.copy(result[:], motion[:])
-            nc.sync.dma_start(out[:, a * HALF : (a + 1) * HALF], result[:])
+            nc.sync.dma_start(out[:, halves[a]], result[:])

import math
from contextlib import ExitStack

import concourse.mybir as mybir

K, T, S, N, H = 1024, 2048, 512, 128, 512
FLOPS = 2 * (2 * K * H * S + H * N * S)

F32 = mybir.dt.float32
BF16 = mybir.dt.bfloat16
I32 = mybir.dt.int32
U32 = mybir.dt.uint32
U16 = mybir.dt.uint16
U8 = mybir.dt.uint8
FP8X4 = mybir.dt.float8_e4m3fn_x4
ALU = mybir.AluOpType
ACT = mybir.ActivationFunctionType

P = 128
PACK = 4
PASSES = K // (P * PACK)
TILES = H // P
QUADRANT = 32
PLANE_ROWS = 4
LIST_ROWS = 16
HALF = S // 2
RUN = 4
EARLY = 2
ROOT = (1.0 + math.sqrt(1.0 - 0.7 * 0.7)) / 0.7


def tile_picked_yfbflo_fix_p_kernel(
    tc, x_words, x_scales, w1, w2, unit, w3, offs, wrp, wr2, out
):
    nc = tc.nc
    with ExitStack() as ctx:
        keep = ctx.enter_context(tc.tile_pool(name="keep", bufs=1))
        psum = ctx.enter_context(tc.psum_pool(name="psum", bufs=1))

        offs_sb = keep.tile([P, S // LIST_ROWS], U16, name="offs_sb")
        wrp_sb = keep.tile([P, S // LIST_ROWS], U16, name="wrp_sb")
        wr2_sb = keep.tile([P, S // LIST_ROWS], U16, name="wr2_sb")
        table_words = [keep.tile([P, T], I32, name="table_words%d" % g) for g in range(PASSES)]
        table_scales = keep.tile([P, T], U8, name="table_scales")

        def load_words(g):
            nc.sync.dma_start(table_words[g][:], x_words[g].rearrange("p c r -> p (c r)").bitcast(I32))

        def load_weight(w, name, g, c0, c1):
            raw = keep.tile([P, PACK, c1 - c0], F32, name="raw_%s_%d_%d" % (name, g, c0), align_bytes=64)
            rows = w[g * P * PACK : (g + 1) * P * PACK, :].rearrange("(p j) c -> p j c", j=PACK)
            nc.sync.dma_start(raw[:], rows[:, :, c0:c1])
            return raw

        def load_halves(w, name, g):
            return [load_weight(w, name, g, c0, c0 + H // 2) for c0 in (0, H // 2)]

        nc.vector.memset(table_scales[:].bitcast(I32), 0)
        load_words(0)
        nc.sync.dma_start(offs_sb[:], offs)
        for q in range(P // QUADRANT):
            nc.sync.dma_start(
                table_scales[QUADRANT * q : QUADRANT * q + PLANE_ROWS * PASSES, :].bitcast(I32),
                x_scales[:, PLANE_ROWS * q : PLANE_ROWS * (q + 1), :].bitcast(I32),
            )
        w1_first = [load_weight(w1, "w1", 0, 0, H)]
        load_words(1)
        w1_last = load_halves(w1, "w1", 1)
        nc.sync.dma_start(wr2_sb[:], wr2)
        w2_first = load_halves(w2, "w2", 0)
        nc.sync.dma_start(wrp_sb[:], wrp)
        w2_last = load_halves(w2, "w2", 1)
        unit_sb = keep.tile([P, TILES], F32, name="unit_sb")
        nc.sync.dma_start(unit_sb[:], unit.rearrange("(p t) o -> p (t o)", t=TILES))
        w3_raw = load_weight(w3, "w3", 0, 0, N)

        x_codes = [keep.tile([P, S], U32, name="x_codes%d" % g, align_bytes=64) for g in range(PASSES)]
        x_planes = keep.tile([P, S], U8, name="x_planes", align_bytes=64)

        def mx_tiles(name, width):
            codes = keep.tile([P, width], U32, name=name + "_codes", align_bytes=64)
            plane = keep.tile([P, width], U8, name=name + "_plane", align_bytes=64)
            return codes, plane

        def quantise(mx, c0, c1, values):
            codes, plane = mx
            nc.vector.quantize_mx(out=codes[:, c0:c1].bitcast(FP8X4), scales=plane[:, c0:c1], in_=values)

        def gather_words(g):
            nc.vector.tensor_copy(x_codes[g][:], table_words[g][:].bitcast(U32).indirect(offs_sb[:]))

        def deal(raws, name):
            dealt = keep.tile([P, TILES, P, PACK], BF16, name=name, align_bytes=64)
            share = P // len(raws)
            for a, raw in enumerate(raws):
                nc.vector.tensor_copy(
                    dealt[:, :, a * share : (a + 1) * share, :].rearrange("p t m j -> p m j t"),
                    raw[:].rearrange("p j (m t) -> p m j t", t=TILES),
                )
            return dealt

        def product_pass(bank, w_mx, t, g):
            codes, plane = w_mx
            cols = slice(t * P, (t + 1) * P)
            nc.tensor.matmul_mx(
                out=bank[:],
                lhsT=codes[:, cols].bitcast(FP8X4),
                lhsT_scale=plane[:, cols],
                rhs=x_codes[g][:].bitcast(FP8X4),
                rhs_scale=x_planes[PLANE_ROWS * g :, :],
                start=(g == 0),
                stop=(g == PASSES - 1),
            )

        def first_pass(raws, name, banks):
            dealt = deal(raws, name + "_dealt0")
            mx = mx_tiles(name + "_0", H)
            quantise(mx, 0, H, dealt[:].rearrange("p t m j -> p (t m j)"))
            for t in range(TILES):
                product_pass(banks[t], mx, t, 0)

        def last_pass(raws, name, banks):
            dealt = deal(raws, name + "_dealt1")
            mx = mx_tiles(name + "_1", H)
            for t in range(TILES):
                quantise(mx, t * P, (t + 1) * P, dealt[:, t].rearrange("p m j -> p (m j)"))
                product_pass(banks[t], mx, t, 1)

        def row_tile(name, t, tag=None):
            name = "%s%d" % (name, t)
            return keep.tile([P, S], F32, name=name, tag=tag or name, align_bytes=64)

        fu = [psum.tile([P, S], F32, name="fu%d" % t, tag="bank%d" % t) for t in range(TILES)]
        bu = [psum.tile([P, S], F32, name="bu%d" % t, tag="bank%d" % (TILES + t)) for t in range(TILES)]

        nc.vector.tensor_copy(x_planes[:], table_scales[:].indirect(offs_sb[:]))
        gather_words(0)
        first_pass(w1_first, "w1", fu)
        gather_words(1)
        last_pass(w1_last, "w1", fu)

        fw = [row_tile("fw", t) for t in range(TILES)]
        for t in range(TILES):
            nc.scalar.activation(fw[t][:], fu[t][:], ACT.Tanh)

        first_pass(w2_first, "w2", bu)
        last_pass(w2_last, "w2", bu)

        half_unit = keep.tile([P, TILES], F32, name="half_unit")
        nc.vector.tensor_scalar(half_unit[:], unit_sb[:], 0.5, None, ALU.mult)

        whole = slice(0, S)
        halves = (slice(0, HALF), slice(HALF, S))
        last = TILES - 1
        f2, gap, tau, swing = {}, {}, {}, {}
        hid = [keep.tile([P, TILES, HALF], BF16, name="hid%d" % a) for a in range(2)]

        def scalar_fetch(dst, picked):
            nc.scalar.activation(dst, picked, ACT.Copy)

        def fetch(dst, window, places, copies):
            width = HALF // LIST_ROWS
            for a, copy in enumerate(copies):
                copy(dst[:, halves[a]], window[:].indirect(places[:, a * width : (a + 1) * width]))

        def stand_in(t, tag, difference):
            f2[t] = row_tile("f2", t, tag)
            fetch(f2[t], fw[t], wr2_sb, (scalar_fetch, scalar_fetch))
            gap[t] = difference
            nc.vector.scalar_tensor_tensor(gap[t][:, whole], fw[t][:], -2.0, f2[t][:], ALU.mult, ALU.add)

        def occlusion(t, bw, parts):
            lead, trail, form = row_tile("lead", t), row_tile("trail", t), row_tile("form", t)
            tau[t] = row_tile("tau", t)
            for cols in parts:
                nc.vector.scalar_tensor_tensor(lead[:, cols], bw[:, cols], ROOT, fw[t][:, cols], ALU.mult, ALU.add)
                nc.vector.scalar_tensor_tensor(trail[:, cols], bw[:, cols], 1.0 / ROOT, fw[t][:, cols], ALU.mult, ALU.add)
                nc.vector.tensor_tensor(form[:, cols], lead[:, cols], trail[:, cols], ALU.mult)
                nc.scalar.activation(tau[t][:, cols], form[:, cols], ACT.Tanh, scale=1.4, bias=-0.4)

        def gate(t, cols):
            nc.vector.scalar_tensor_tensor(
                swing[t][:, cols], gap[t][:, cols], half_unit[:, t : t + 1], tau[t][:, cols], ALU.mult, ALU.mult
            )

        def repair(t, a):
            nc.vector.scalar_tensor_tensor(
                hid[a][:, t, :], f2[t][:, halves[a]], half_unit[:, t : t + 1], swing[t][:, halves[a]], ALU.mult, ALU.add
            )

        early_gaps = keep.tile([P, EARLY, S], F32, name="early_gaps", tag="w2_dealt1", align_bytes=64)
        for t in range(EARLY):
            stand_in(t, None, early_gaps[:, t, :])

        bv_tags = ["bv%d" % t if t < EARLY else "form%d" % (t - EARLY) for t in range(TILES)]
        for t in range(TILES):
            bv = row_tile("bv", t, bv_tags[t])
            nc.scalar.activation(bv[:], bu[t][:], ACT.Tanh)
            bw = row_tile("bw", t)
            fetch(bw, bv, wrp_sb, (scalar_fetch, nc.vector.tensor_copy if t == 0 else scalar_fetch))
            occlusion(t, bw, halves if t == last else (whole,))
            if t >= EARLY:
                stand_in(t, bv_tags[t - 1], row_tile("gap", t))
            swing[t] = row_tile("swing", t)
            if 0 < t < last:
                gate(t - 1, whole)
                repair(t - 1, 0)
                repair(t - 1, 1)

        def interleave(copy, dst, src):
            copy(dst.rearrange("p (c i) j -> p c j i", i=RUN), src.rearrange("p j (c i) -> p c j i", i=RUN))

        w3_grouped = keep.tile([P, N, PACK], BF16, name="w3_grouped", tag="bw1", align_bytes=64)
        interleave(nc.scalar.copy, w3_grouped[:], w3_raw[:])
        w3_mx = mx_tiles("w3", N)
        quantise(w3_mx, 0, N, w3_grouped[:].rearrange("p n j -> p (n j)"))

        woven = [keep.tile([P, HALF, TILES], BF16, name="woven%d" % a, align_bytes=64) for a in range(2)]
        gate(last - 1, whole)
        for a, copy in enumerate((nc.scalar.copy, nc.vector.tensor_copy)):
            gate(last, halves[a])
            repair(last - 1, a)
            repair(last, a)
            interleave(copy, woven[a][:], hid[a][:])

        for a in range(2):
            hid_mx = mx_tiles("hid%d" % a, HALF)
            quantise(hid_mx, 0, HALF, woven[a][:].rearrange("p c t -> p (c t)"))
            motion = psum.tile([P, HALF], F32, name="motion%d" % a, tag="bank%d" % a)
            nc.tensor.matmul_mx(
                out=motion[:],
                lhsT=w3_mx[0][:].bitcast(FP8X4),
                lhsT_scale=w3_mx[1][:],
                rhs=hid_mx[0][:].bitcast(FP8X4),
                rhs_scale=hid_mx[1][:],
                start=True,
                stop=True,
            )
            result = keep.tile([P, HALF], F32, name="result%d" % a)
            nc.scalar.copy(result[:], motion[:])
            nc.sync.dma_start(out[:, halves[a]], result[:])
